import numpy as np
import ml_dtypes


def mxq(x, axis, fmt="e4m3"):
    dtype, down = {"e4m3": (ml_dtypes.float8_e4m3fn, 7), "e5m2": (ml_dtypes.float8_e5m2, 14)}[fmt]
    v = np.moveaxis(np.asarray(x, np.float32).astype(ml_dtypes.bfloat16).astype(np.float64), axis, -1)
    blocks = v.reshape(v.shape[:-1] + (-1, 32))
    amax = np.abs(blocks).max(-1, keepdims=True)
    byte = np.maximum(np.where(amax > 0, np.frexp(amax)[1] - 1 + 127, 0) - down, 1)
    scale = np.exp2(byte - 127.0)
    codes = (blocks / scale).astype(np.float32).astype(dtype).astype(np.float64)
    return np.moveaxis((codes * scale).reshape(v.shape), -1, axis)


WIDE = False


def mx_kscale(k):
    if not WIDE:
        return np.ones(k)
    levels = np.array([10, -10, 5, -5, 0])
    if k % 512:
        return np.exp2(np.random.permutation(np.resize(levels, k // 32))).repeat(32)
    a = np.empty((k // 512, 16))
    for p in range(k // 512):
        a[p, :8] = np.random.permutation(np.resize(levels, 8))
        for g in range(8):
            far = levels[np.abs(levels - a[p, g]) >= 10]
            a[p, g + 8] = far[np.random.randint(len(far))]
    return np.exp2(a.ravel()).repeat(32)


BF16 = ml_dtypes.bfloat16


def bf(x):
    return np.asarray(x, np.float32).astype(BF16)


def f64(x):
    return np.asarray(x).astype(np.float64)


E2M1 = np.array([0.0, 0.5, 1.0, 1.5, 2.0, 3.0, 4.0, 6.0, -0.0, -0.5, -1.0, -1.5, -2.0, -3.0, -4.0, -6.0])


def pack_weight(w, fmt):
    k, n = w.shape
    w = f64(bf(w)).reshape(k // 32, 32, n)
    amax = np.abs(w).max(1)
    if fmt == "e4m3":
        byte = np.frexp(amax)[1] - 1 + 127 - 7
    else:
        mant, ex = np.frexp(amax / 6.0)
        byte = np.where(mant > 0.5, ex, ex - 1) + 127
    byte = np.clip(np.where(amax > 0, byte, 1), 1, 254)
    scaled = (w * np.exp2(127.0 - byte)[:, None, :]).reshape(k, n).astype(np.float32)
    by_word = np.ascontiguousarray(scaled.reshape(k // 512, 128, 4, n).transpose(0, 1, 3, 2))
    if fmt == "e4m3":
        words = by_word.astype(ml_dtypes.float8_e4m3fn).view(np.uint8)
    else:
        c = by_word.astype(ml_dtypes.float4_e2m1fn).view(np.uint8) & 0xF
        words = c[..., 0::2] | (c[..., 1::2] << 4)
    return np.ascontiguousarray(words), np.ascontiguousarray(byte.astype(np.uint8).reshape(k // 512, 16, n))


def unpack_weight(words, scales, fmt):
    g, p, n, _ = words.shape
    if fmt == "e4m3":
        vals = np.ascontiguousarray(words).view(ml_dtypes.float8_e4m3fn).astype(np.float64)
    else:
        nib = np.empty((g, p, n, 4), np.uint8)
        nib[..., 0::2] = words & 0xF
        nib[..., 1::2] = words >> 4
        vals = E2M1[nib]
    vals = vals * np.repeat(np.exp2(scales.astype(np.float64) - 127.0), 8, axis=1)[..., None]
    return vals.transpose(0, 1, 3, 2).reshape(g * 512, n)
def pack4(w):
    words, scales = pack_weight(w, "e2m1")
    return words.reshape(words.shape[0], 128, -1), scales


def unpack4(words, scales):
    return unpack_weight(words.reshape(words.shape[0], 128, -1, 2), scales, "e2m1")


def planes(Y):
    n, m = Y.shape
    b = f64(bf(Y)).reshape(n // 32, 32, m)
    amax = np.abs(b).max(1)
    byte = np.clip(np.where(amax > 0, np.frexp(amax)[1] - 1 + 127 - 7, 1), 1, 254)
    codes = (b * np.exp2(127.0 - byte)[:, None, :]).reshape(n, m).astype(np.float32).astype(ml_dtypes.float8_e4m3fn).view(np.uint8)
    words = codes.reshape(n // 512, 128, 4, m).transpose(0, 1, 3, 2)
    return np.ascontiguousarray(words), np.ascontiguousarray(byte.astype(np.uint8).reshape(n // 512, 16, m))


M, K, N = 2048, 1536, 1024
SHIFT_SCALE = 0.3
TAU_SPREAD = 0.4
TAU_CENTRE = -0.3

def setup_inputs():
    s = mx_kscale(K)
    x = np.random.randn(K, M) * s[:, None]
    x_words, x_scales = pack_weight(x, "e4m3")
    spread = np.exp(0.8 * np.random.randn(N))
    w = np.random.randn(K, N) / np.sqrt(K) * spread[None, :] / s[:, None]
    shift = SHIFT_SCALE * np.random.randn(N) * spread
    log_tau = TAU_CENTRE + TAU_SPREAD * np.random.randn(M)
    return {"x_words": x_words, "x_scales": x_scales, "w": bf(w),
            "shift": bf(shift), "log_tau": bf(log_tau)}

def reference(x_words, x_scales, w, shift, log_tau):
    X = unpack_weight(x_words, x_scales, "e4m3")
    W = mxq(f64(w), 0, "e4m3")
    e = X.T @ W
    y = (e + f64(shift)[None, :]) / np.exp(f64(log_tau))[:, None]
    Y = y.T
    words, scales = planes(Y)
    return y, words, scales

@@ -1,0 +1,282 @@
+from contextlib import ExitStack
+
+import concourse.mybir as mybir
+from concourse.masks import make_identity
+
+M, K, N = 2048, 1536, 1024
+FLOPS = 2 * M * K * N
+
+F32 = mybir.dt.float32
+BF16 = mybir.dt.bfloat16
+I32 = mybir.dt.int32
+U32 = mybir.dt.uint32
+U8 = mybir.dt.uint8
+FP8X4 = mybir.dt.float8_e4m3fn_x4
+ACT = mybir.ActivationFunctionType
+ALU = mybir.AluOpType
+
+P = 128
+PACK = 4
+K_PASS = P * PACK
+PASSES = K // K_PASS
+HALF = 512
+HALVES = N // HALF
+TILES = M // P
+UNITS = TILES * HALVES
+CHUNK = 512
+CHUNKS = M // CHUNK
+TILES_PER_CHUNK = CHUNK // P
+
+HEAD_VECTOR_COLS = 256
+MM_AHEAD = 3
+SHR_AHEAD = 3
+LATE_VECTOR_COLS = 128
+SLOW, FAST, FIRST, CATCH = 5, 3, 7, 10
+GP_MOD = ()
+SC_TAIL = ()
+FIRST_COLS = 256
+SC_CAST_FROM = 99
+SC_CAST_EVERY = 2
+
+
+def tile_caption_projection_over_temperature_g6_kernel(
+    tc, x_words, x_scales, w, shift, log_tau, out_0, out_1, out_2
+):
+    nc = tc.nc
+    with ExitStack() as ctx:
+        keep = ctx.enter_context(tc.tile_pool(name="keep", bufs=1))
+        flow = ctx.enter_context(tc.tile_pool(name="flow", bufs=3))
+        acc_pool = ctx.enter_context(tc.psum_pool(name="acc", bufs=6))
+        turn_pool = ctx.enter_context(tc.psum_pool(name="turn", bufs=2))
+        ctx.enter_context(tc.manual_schedule())
+
+        plane_first = keep.tile([P, CHUNK], U8, align_bytes=64)
+        plane_rest = keep.tile([P, M - CHUNK], U8, align_bytes=64)
+        nc.vector.memset(plane_first[:].bitcast(I32), 0)
+        nc.vector.memset(plane_rest[:].bitcast(I32), 0)
+
+        def load_scales(queue, plane, lo, hi):
+            for q in range(4):
+                queue.dma_start(
+                    out=plane[32 * q : 32 * q + 4 * PASSES, :].bitcast(I32),
+                    in_=x_scales[:, 4 * q : 4 * q + 4, lo:hi].bitcast(I32),
+                )
+
+        r_rows = keep.tile([P, P], F32)
+        tau_rows = keep.tile([TILES, P], BF16)
+        nc.scalar.dma_start(out=tau_rows[:], in_=log_tau.rearrange("(i p) -> i p", p=P))
+        shift_cols = keep.tile([P, N // P], BF16)
+        nc.scalar.dma_start(out=shift_cols[:], in_=shift.rearrange("(p a) -> p a", p=P))
+        ident = keep.tile([P, P], F32)
+        make_identity(nc, ident[:])
+        nc.scalar.activation(out=r_rows[:], in_=ident[:], func=ACT.Exp)
+
+        w_raw, x_codes = {}, {}
+
+        def load_w(g, h):
+            raw = keep.tile([P, PACK, HALF], BF16, name="w_raw_%d_%d" % (g, h))
+            rows = w[g * K_PASS : (g + 1) * K_PASS, h * HALF : (h + 1) * HALF]
+            nc.sync.dma_start(out=raw[:], in_=rows.rearrange("(p j) n -> p j n", j=PACK))
+            w_raw[g, h] = raw
+
+        def load_x(c, g_lo, g_hi):
+            words = keep.tile([P, g_hi - g_lo, CHUNK], U32, name="x_codes_%d_%d" % (c, g_lo), align_bytes=64)
+            src = x_words.rearrange("g p n t -> p g (n t)")[:, g_lo:g_hi, c * CHUNK * PACK : (c + 1) * CHUNK * PACK]
+            nc.sync.dma_start(out=words[:].bitcast(I32), in_=src.bitcast(I32))
+            for g in range(g_lo, g_hi):
+                x_codes[c, g] = words[:, g - g_lo, :]
+
+        load_w(0, 0)
+        load_x(0, 0, 1)
+        load_w(1, 0)
+        load_scales(nc.sync, plane_first, 0, CHUNK)
+        load_x(0, 1, 2)
+        load_w(2, 0)
+        load_x(0, 2, 3)
+        load_x(1, 0, PASSES)
+        load_scales(nc.sync, plane_rest, CHUNK, M)
+        load_w(0, 1)
+        load_w(1, 1)
+        load_x(2, 0, PASSES)
+        load_w(2, 1)
+        load_x(3, 0, PASSES)
+
+        w_grouped, w_codes, w_plane = {}, {}, {}
+
+        def interleave_w(copy, g, h, lo, hi):
+            if (g, h) not in w_grouped:
+                w_grouped[g, h] = flow.tile([P, HALF, PACK], BF16, name="w_grouped", align_bytes=64)
+            copy(
+                out=w_grouped[g, h][:, lo:hi, :].rearrange("p (c i) t -> p c t i", i=4),
+                in_=w_raw[g, h][:, :, lo:hi].rearrange("p t (c i) -> p c t i", i=4),
+            )
+
+        def quantize_w(g, h):
+            codes = keep.tile([P, HALF], U32, name="w_codes_%d_%d" % (g, h), align_bytes=64)
+            plane = keep.tile([P, HALF], U8, name="w_plane_%d_%d" % (g, h), align_bytes=64)
+            nc.vector.quantize_mx(
+                out=codes[:].bitcast(FP8X4), scales=plane[:], in_=w_grouped[g, h][:].rearrange("p n t -> p (n t)")
+            )
+            w_codes[g, h], w_plane[g, h] = codes, plane
+
+        acc = {}
+
+        def mm_pass(u, g):
+            h, i = divmod(u, TILES)
+            if g == 0:
+                acc[u] = acc_pool.tile([P, HALF], F32, name="acc")
+            c, t = divmod(i, TILES_PER_CHUNK)
+            plane, col = (plane_first, i * P) if c == 0 else (plane_rest, i * P - CHUNK)
+            nc.tensor.matmul_mx(
+                out=acc[u][:],
+                lhsT=x_codes[c, g][:, t * P : (t + 1) * P].bitcast(FP8X4),
+                lhsT_scale=plane[4 * g :, col : col + P],
+                rhs=w_codes[g, h][:].bitcast(FP8X4),
+                rhs_scale=w_plane[g, h][:],
+                start=(g == 0),
+                stop=(g == PASSES - 1),
+            )
+
+        def head_w(g):
+            cols = FIRST_COLS if g == 0 else HEAD_VECTOR_COLS
+            interleave_w(nc.vector.tensor_copy, g, 0, 0, cols)
+            if cols < HALF:
+                interleave_w(nc.scalar.copy, g, 0, cols, HALF)
+
+        nc.scalar.activation(out=r_rows[:TILES, :], in_=tau_rows[:], func=ACT.Exp, scale=-1.0)
+        shift_bank = turn_pool.tile([P, PACK, P], F32, name="turned")
+        for a in range(PACK):
+            word = shift_cols[:].bitcast(F32)[:, a : a + 1]
+            nc.tensor.transpose(shift_bank[:, a, :], word.to_broadcast([P, P]), ident[:])
+        r_bank = turn_pool.tile([P, PACK, P], F32, name="turned")
+        nc.tensor.transpose(r_bank[:, 0, :], r_rows[:], ident[:])
+        r = keep.tile([P, TILES], F32)
+        shift_all = keep.tile([P, N], BF16)
+
+        shr = {}
+
+        def scale_shift(u):
+            h, i = divmod(u, TILES)
+            shr[u] = flow.tile([P, HALF], F32, name="shr", bufs=SHR_AHEAD + 2)
+            src = shift_all[:, h * HALF : (h + 1) * HALF]
+            if u % 4 in GP_MOD and u >= 4:
+                nc.gpsimd.tensor_scalar(
+                    out=shr[u][:], in0=src, scalar1=r[:, i : i + 1], scalar2=0.0, op0=ALU.mult, op1=ALU.add
+                )
+            else:
+                nc.scalar.activation(out=shr[u][:], in_=src, func=ACT.Copy, scale=r[:, i : i + 1])
+
+        for g in range(PASSES):
+            head_w(g)
+            if g == 1:
+                nc.vector.tensor_copy(out=r[:], in_=r_bank[:, 0, :TILES])
+            quantize_w(g, 0)
+            if g == 1:
+                nc.vector.tensor_copy(out=shift_all[:].bitcast(F32), in_=shift_bank[:].rearrange("p a n -> p n a"))
+            for u in range(TILES_PER_CHUNK):
+                mm_pass(u, g)
+        for u in range(SHR_AHEAD):
+            scale_shift(u)
+
+        pieces = [(u, u + 1) for u in range(0, UNITS - 2, 2)] + [(UNITS - 2,), (UNITS - 1,)]
+        piece_of = {u: piece for piece in pieces for u in piece}
+        batches = [tuple(pieces[b : b + 2]) for b in range(0, len(pieces) - 3, 2)] + [(piece,) for piece in pieces[-3:]]
+        y_tile, y_words, banks, y_turned = {}, {}, {}, {}
+        y_codes = [keep.tile([P, M], U32, name="y_codes_%d" % h, align_bytes=64) for h in range(HALVES)]
+        y_plane = [keep.tile([P, M], U8, name="y_plane_%d" % h, align_bytes=64) for h in range(HALVES)]
+
+        def epilogue(u):
+            h, i = divmod(u, TILES)
+            piece = piece_of[u]
+            if u == piece[0]:
+                y_tile[piece] = flow.tile([P, len(piece), HALF], F32, name="y", bufs=8)
+            nc.vector.scalar_tensor_tensor(
+                out=y_tile[piece][:, u - piece[0], :], in0=acc[u][:], scalar=r[:, i : i + 1], in1=shr[u][:],
+                op0=ALU.mult, op1=ALU.add,
+            )
+            if u == piece[-1]:
+                first = piece[0] % TILES
+                dst = out_0[first * P : (first + len(piece)) * P, h * HALF : (h + 1) * HALF]
+                nc.sync.dma_start(out=dst.rearrange("(t p) n -> p t n", p=P), in_=y_tile[piece][:])
+
+        def round_y(piece):
+            y_words[piece] = flow.tile([P, len(piece), HALF], BF16, name="y_words", bufs=8)
+            on_scalar = piece[0] >= SC_CAST_FROM and (piece[0] // 2) % SC_CAST_EVERY == 0 and len(piece) == 2 or piece[0] in SC_TAIL
+            copy = nc.scalar.copy if on_scalar else nc.vector.tensor_copy
+            copy(
+                out=y_words[piece][:].rearrange("c t (u p e) -> c t u p e", u=2, e=2),
+                in_=y_tile[piece][:].rearrange("c t (p u e) -> c t u p e", u=2, e=2),
+            )
+
+        def turn(batch):
+            for piece in batch:
+                banks[piece] = turn_pool.tile([P, len(piece), 2, P], F32, name="turned")
+                words = y_words[piece][:].bitcast(F32)
+                for t in range(len(piece)):
+                    for u in range(2):
+                        nc.tensor.transpose(banks[piece][:, t, u, :], words[:, t, u * P : (u + 1) * P], ident[:])
+
+        def copy_out(batch, k):
+            piece = batch[k]
+            if k == 0:
+                tiles = sum(len(x) for x in batch)
+                y_turned[batch] = flow.tile([P, tiles * P * PACK], BF16, name="y_turned", bufs=3, align_bytes=64)
+            width = len(piece) * P * 2
+            dst = y_turned[batch][:].bitcast(F32)[:, k * width : (k + 1) * width]
+            nc.scalar.copy(
+                out=dst.rearrange("p (t c u) -> p t c u", c=P, u=2), in_=banks[piece][:].rearrange("p t u c -> p t c u")
+            )
+
+        def quantize_y(batch):
+            h, i = divmod(batch[0][0], TILES)
+            last = batch[-1][-1] % TILES
+            cols = slice(i * P, (last + 1) * P)
+            nc.vector.quantize_mx(
+                out=y_codes[h][:, cols].bitcast(FP8X4), scales=y_plane[h][:, cols], in_=y_turned[batch][:]
+            )
+            dst = out_1[h].rearrange("p m t -> p (m t)")[:, cols.start * PACK : cols.stop * PACK]
+            nc.sync.dma_start(out=dst.bitcast(I32), in_=y_codes[h][:, cols].bitcast(I32))
+
+        def store_scales(h, lo, hi, queues):
+            for q in range(4):
+                queues[q % len(queues)].dma_start(
+                    out=out_2[h, 4 * q : 4 * q + 4, lo:hi].bitcast(I32),
+                    in_=y_plane[h][32 * q : 32 * q + 4, lo:hi].bitcast(I32),
+                )
+
+        full = [b for b in batches if len(b) == 2]
+        turn_step = {max(4 * n + 4, min(SLOW * n + FIRST, FAST * n + CATCH)): b for n, b in enumerate(full)}
+        for n, b in enumerate(batches[len(full) :]):
+            turn_step[UNITS - 2 + n] = b
+        assert len(turn_step) == len(batches)
+
+        for s in range(UNITS + 4):
+            if s + SHR_AHEAD < UNITS:
+                scale_shift(s + SHR_AHEAD)
+            if 2 <= s <= 12 and s % 2 == 0:
+                g, part = divmod(s // 2 - 1, 2)
+                width = (HALF - LATE_VECTOR_COLS) // 2
+                interleave_w(nc.scalar.copy, g, 1, part * width, (part + 1) * width)
+            if s < UNITS:
+                epilogue(s)
+            if s in (3, 7, 11) and LATE_VECTOR_COLS:
+                interleave_w(nc.vector.tensor_copy, (s - 3) // 4, 1, HALF - LATE_VECTOR_COLS, HALF)
+            if s in (5, 9, 13):
+                quantize_w((s - 5) // 4, 1)
+            if 1 <= s <= UNITS and s - 1 == piece_of[s - 1][-1]:
+                round_y(piece_of[s - 1])
+            if TILES_PER_CHUNK <= s + MM_AHEAD < UNITS:
+                for g in range(PASSES):
+                    mm_pass(s + MM_AHEAD, g)
+            for lag in (2, 1):
+                b = turn_step.get(s - lag)
+                if b is not None and lag - 1 < len(b):
+                    copy_out(b, lag - 1)
+            if s in turn_step:
+                turn(turn_step[s])
+            b = turn_step.get(s - 3)
+            if b is not None:
+                quantize_y(b)
+                if b[-1][-1] == TILES - 1:
+                    store_scales(0, 0, M, [nc.sync])
+        store_scales(1, 0, M, [nc.sync, nc.scalar])

@@ -17,6 +17,7 @@ ALU = mybir.AluOpType
 
 P = 128
 PACK = 4
+QUADRANTS = 4
 K_PASS = P * PACK
 PASSES = K // K_PASS
 HALF = 512
@@ -24,19 +25,17 @@ HALVES = N // HALF
 TILES = M // P
 UNITS = TILES * HALVES
 CHUNK = 512
-CHUNKS = M // CHUNK
-TILES_PER_CHUNK = CHUNK // P
+CHUNK_TILES = CHUNK // P
+MX_ALIGN = 256
 
-HEAD_VECTOR_COLS = 256
-MM_AHEAD = 3
+ACC_BANKS = 6
+MM_AHEAD = 2
 SHR_AHEAD = 3
-LATE_VECTOR_COLS = 128
-SLOW, FAST, FIRST, CATCH = 5, 3, 7, 10
-GP_MOD = ()
-SC_TAIL = ()
-FIRST_COLS = 256
-SC_CAST_FROM = 99
-SC_CAST_EVERY = 2
+SHR_BUFS = SHR_AHEAD + 2
+HEAD_VECTOR_COLS = (256, 256, 320)
+W_LATE_FROM = 5
+FIRST_RUN_STEP = 5
+RUN_SPACING = 3
 
 
 def tile_caption_projection_over_temperature_g6_kernel(
@@ -46,18 +45,18 @@ def tile_caption_projection_over_temperature_g6_kernel(
     with ExitStack() as ctx:
         keep = ctx.enter_context(tc.tile_pool(name="keep", bufs=1))
         flow = ctx.enter_context(tc.tile_pool(name="flow", bufs=3))
-        acc_pool = ctx.enter_context(tc.psum_pool(name="acc", bufs=6))
-        turn_pool = ctx.enter_context(tc.psum_pool(name="turn", bufs=2))
+        acc_pool = ctx.enter_context(tc.psum_pool(name="acc", bufs=ACC_BANKS))
+        turn_pool = ctx.enter_context(tc.psum_pool(name="turn", bufs=8 - ACC_BANKS))
         ctx.enter_context(tc.manual_schedule())
 
-        plane_first = keep.tile([P, CHUNK], U8, align_bytes=64)
-        plane_rest = keep.tile([P, M - CHUNK], U8, align_bytes=64)
+        plane_first = keep.tile([P, CHUNK], U8, align_bytes=MX_ALIGN)
+        plane_rest = keep.tile([P, M - CHUNK], U8, align_bytes=MX_ALIGN)
         nc.vector.memset(plane_first[:].bitcast(I32), 0)
         nc.vector.memset(plane_rest[:].bitcast(I32), 0)
 
-        def load_scales(queue, plane, lo, hi):
-            for q in range(4):
-                queue.dma_start(
+        def load_scales(plane, lo, hi):
+            for q in range(QUADRANTS):
+                nc.sync.dma_start(
                     out=plane[32 * q : 32 * q + 4 * PASSES, :].bitcast(I32),
                     in_=x_scales[:, 4 * q : 4 * q + 4, lo:hi].bitcast(I32),
                 )
@@ -76,44 +75,44 @@ def tile_caption_projection_over_temperature_g6_kernel(
         def load_w(g, h):
             raw = keep.tile([P, PACK, HALF], BF16, name="w_raw_%d_%d" % (g, h))
             rows = w[g * K_PASS : (g + 1) * K_PASS, h * HALF : (h + 1) * HALF]
-            nc.sync.dma_start(out=raw[:], in_=rows.rearrange("(p j) n -> p j n", j=PACK))
+            nc.sync.dma_start(out=raw[:], in_=rows.rearrange("(p t) n -> p t n", t=PACK))
             w_raw[g, h] = raw
 
         def load_x(c, g_lo, g_hi):
-            words = keep.tile([P, g_hi - g_lo, CHUNK], U32, name="x_codes_%d_%d" % (c, g_lo), align_bytes=64)
+            words = keep.tile([P, g_hi - g_lo, CHUNK], U32, name="x_codes_%d_%d" % (c, g_lo), align_bytes=MX_ALIGN)
             src = x_words.rearrange("g p n t -> p g (n t)")[:, g_lo:g_hi, c * CHUNK * PACK : (c + 1) * CHUNK * PACK]
             nc.sync.dma_start(out=words[:].bitcast(I32), in_=src.bitcast(I32))
             for g in range(g_lo, g_hi):
                 x_codes[c, g] = words[:, g - g_lo, :]
 
         load_w(0, 0)
-        load_x(0, 0, 1)
         load_w(1, 0)
-        load_scales(nc.sync, plane_first, 0, CHUNK)
-        load_x(0, 1, 2)
+        load_x(0, 0, 1)
+        load_scales(plane_first, 0, CHUNK)
         load_w(2, 0)
+        load_x(0, 1, 2)
         load_x(0, 2, 3)
         load_x(1, 0, PASSES)
-        load_scales(nc.sync, plane_rest, CHUNK, M)
+        load_scales(plane_rest, CHUNK, M)
         load_w(0, 1)
-        load_w(1, 1)
         load_x(2, 0, PASSES)
-        load_w(2, 1)
+        load_w(1, 1)
         load_x(3, 0, PASSES)
+        load_w(2, 1)
 
         w_grouped, w_codes, w_plane = {}, {}, {}
 
         def interleave_w(copy, g, h, lo, hi):
-            if (g, h) not in w_grouped:
-                w_grouped[g, h] = flow.tile([P, HALF, PACK], BF16, name="w_grouped", align_bytes=64)
+            if lo == 0:
+                w_grouped[g, h] = flow.tile([P, HALF, PACK], BF16, name="w_grouped", align_bytes=MX_ALIGN)
             copy(
-                out=w_grouped[g, h][:, lo:hi, :].rearrange("p (c i) t -> p c t i", i=4),
-                in_=w_raw[g, h][:, :, lo:hi].rearrange("p t (c i) -> p c t i", i=4),
+                out=w_grouped[g, h][:, lo:hi, :].rearrange("p (n i) t -> p n t i", i=4),
+                in_=w_raw[g, h][:, :, lo:hi].rearrange("p t (n i) -> p n t i", i=4),
             )
 
         def quantize_w(g, h):
-            codes = keep.tile([P, HALF], U32, name="w_codes_%d_%d" % (g, h), align_bytes=64)
-            plane = keep.tile([P, HALF], U8, name="w_plane_%d_%d" % (g, h), align_bytes=64)
+            codes = keep.tile([P, HALF], U32, name="w_codes_%d_%d" % (g, h), align_bytes=MX_ALIGN)
+            plane = keep.tile([P, HALF], U8, name="w_plane_%d_%d" % (g, h), align_bytes=MX_ALIGN)
             nc.vector.quantize_mx(
                 out=codes[:].bitcast(FP8X4), scales=plane[:], in_=w_grouped[g, h][:].rearrange("p n t -> p (n t)")
             )
@@ -125,31 +124,25 @@ def tile_caption_projection_over_temperature_g6_kernel(
             h, i = divmod(u, TILES)
             if g == 0:
                 acc[u] = acc_pool.tile([P, HALF], F32, name="acc")
-            c, t = divmod(i, TILES_PER_CHUNK)
-            plane, col = (plane_first, i * P) if c == 0 else (plane_rest, i * P - CHUNK)
+            c, col = divmod(i * P, CHUNK)
+            plane, plane_col = (plane_first, col) if c == 0 else (plane_rest, i * P - CHUNK)
             nc.tensor.matmul_mx(
                 out=acc[u][:],
-                lhsT=x_codes[c, g][:, t * P : (t + 1) * P].bitcast(FP8X4),
-                lhsT_scale=plane[4 * g :, col : col + P],
+                lhsT=x_codes[c, g][:, col : col + P].bitcast(FP8X4),
+                lhsT_scale=plane[4 * g :, plane_col : plane_col + P],
                 rhs=w_codes[g, h][:].bitcast(FP8X4),
                 rhs_scale=w_plane[g, h][:],
                 start=(g == 0),
                 stop=(g == PASSES - 1),
             )
 
-        def head_w(g):
-            cols = FIRST_COLS if g == 0 else HEAD_VECTOR_COLS
-            interleave_w(nc.vector.tensor_copy, g, 0, 0, cols)
-            if cols < HALF:
-                interleave_w(nc.scalar.copy, g, 0, cols, HALF)
-
         nc.scalar.activation(out=r_rows[:TILES, :], in_=tau_rows[:], func=ACT.Exp, scale=-1.0)
-        shift_bank = turn_pool.tile([P, PACK, P], F32, name="turned")
-        for a in range(PACK):
-            word = shift_cols[:].bitcast(F32)[:, a : a + 1]
-            nc.tensor.transpose(shift_bank[:, a, :], word.to_broadcast([P, P]), ident[:])
-        r_bank = turn_pool.tile([P, PACK, P], F32, name="turned")
-        nc.tensor.transpose(r_bank[:, 0, :], r_rows[:], ident[:])
+        shift_words = shift_cols[:].bitcast(F32)
+        shift_bank = turn_pool.tile([P, shift_words.shape[1], P], F32, name="turned")
+        for a in range(shift_words.shape[1]):
+            nc.tensor.transpose(shift_bank[:, a, :], shift_words[:, a : a + 1].to_broadcast([P, P]), ident[:])
+        r_bank = turn_pool.tile([P, P], F32, name="turned")
+        nc.tensor.transpose(r_bank[:], r_rows[:], ident[:])
         r = keep.tile([P, TILES], F32)
         shift_all = keep.tile([P, N], BF16)
 
@@ -157,126 +150,138 @@ def tile_caption_projection_over_temperature_g6_kernel(
 
         def scale_shift(u):
             h, i = divmod(u, TILES)
-            shr[u] = flow.tile([P, HALF], F32, name="shr", bufs=SHR_AHEAD + 2)
+            shr[u] = flow.tile([P, HALF], F32, name="shr", bufs=SHR_BUFS)
             src = shift_all[:, h * HALF : (h + 1) * HALF]
-            if u % 4 in GP_MOD and u >= 4:
+            if u < SHR_BUFS:
+                nc.scalar.activation(out=shr[u][:], in_=src, func=ACT.Copy, scale=r[:, i : i + 1])
+            else:
                 nc.gpsimd.tensor_scalar(
                     out=shr[u][:], in0=src, scalar1=r[:, i : i + 1], scalar2=0.0, op0=ALU.mult, op1=ALU.add
                 )
-            else:
-                nc.scalar.activation(out=shr[u][:], in_=src, func=ACT.Copy, scale=r[:, i : i + 1])
 
         for g in range(PASSES):
-            head_w(g)
+            interleave_w(nc.vector.tensor_copy, g, 0, 0, HEAD_VECTOR_COLS[g])
+            interleave_w(nc.scalar.copy, g, 0, HEAD_VECTOR_COLS[g], HALF)
             if g == 1:
-                nc.vector.tensor_copy(out=r[:], in_=r_bank[:, 0, :TILES])
+                nc.vector.tensor_copy(out=r[:], in_=r_bank[:, :TILES])
             quantize_w(g, 0)
             if g == 1:
-                nc.vector.tensor_copy(out=shift_all[:].bitcast(F32), in_=shift_bank[:].rearrange("p a n -> p n a"))
-            for u in range(TILES_PER_CHUNK):
+                nc.scalar.copy(out=shift_all[:].bitcast(F32), in_=shift_bank[:].rearrange("p a n -> p n a"))
+            for u in range(CHUNK_TILES):
                 mm_pass(u, g)
         for u in range(SHR_AHEAD):
             scale_shift(u)
 
         pieces = [(u, u + 1) for u in range(0, UNITS - 2, 2)] + [(UNITS - 2,), (UNITS - 1,)]
         piece_of = {u: piece for piece in pieces for u in piece}
-        batches = [tuple(pieces[b : b + 2]) for b in range(0, len(pieces) - 3, 2)] + [(piece,) for piece in pieces[-3:]]
+        long_runs = [tuple(pieces[b : b + 2]) for b in range(0, len(pieces) - 3, 2)]
+        short_runs = [(piece,) for piece in pieces[-3:]]
+        span_tiles = [(8, 8), (4, 4, 4, 2, 1, 1)]
+        span_of = {}
+        for h in range(HALVES):
+            first = 0
+            for count in span_tiles[h]:
+                for i in range(first, first + count):
+                    span_of[h, i] = range(first, first + count)
+                first = first + count
+
         y_tile, y_words, banks, y_turned = {}, {}, {}, {}
-        y_codes = [keep.tile([P, M], U32, name="y_codes_%d" % h, align_bytes=64) for h in range(HALVES)]
-        y_plane = [keep.tile([P, M], U8, name="y_plane_%d" % h, align_bytes=64) for h in range(HALVES)]
+        y_codes = [keep.tile([P, M], U32, name="y_codes_%d" % h, align_bytes=MX_ALIGN) for h in range(HALVES)]
+        y_plane = [keep.tile([P, M], U8, name="y_plane_%d" % h, align_bytes=MX_ALIGN) for h in range(HALVES)]
 
         def epilogue(u):
             h, i = divmod(u, TILES)
             piece = piece_of[u]
             if u == piece[0]:
-                y_tile[piece] = flow.tile([P, len(piece), HALF], F32, name="y", bufs=8)
+                y_tile[piece] = keep.tile([P, len(piece), HALF], F32, name="y_%d" % u)
             nc.vector.scalar_tensor_tensor(
                 out=y_tile[piece][:, u - piece[0], :], in0=acc[u][:], scalar=r[:, i : i + 1], in1=shr[u][:],
                 op0=ALU.mult, op1=ALU.add,
             )
             if u == piece[-1]:
-                first = piece[0] % TILES
-                dst = out_0[first * P : (first + len(piece)) * P, h * HALF : (h + 1) * HALF]
-                nc.sync.dma_start(out=dst.rearrange("(t p) n -> p t n", p=P), in_=y_tile[piece][:])
+                dst = out_0[(i + 1 - len(piece)) * P : (i + 1) * P, h * HALF : (h + 1) * HALF]
+                nc.sync.dma_start(out=dst.rearrange("(t c) n -> c t n", c=P), in_=y_tile[piece][:])
 
-        def round_y(piece):
-            y_words[piece] = flow.tile([P, len(piece), HALF], BF16, name="y_words", bufs=8)
-            on_scalar = piece[0] >= SC_CAST_FROM and (piece[0] // 2) % SC_CAST_EVERY == 0 and len(piece) == 2 or piece[0] in SC_TAIL
-            copy = nc.scalar.copy if on_scalar else nc.vector.tensor_copy
+        def round_y(piece, copy):
+            y_words[piece] = flow.tile([P, len(piece), HALF], BF16, name="y_words", bufs=4)
             copy(
-                out=y_words[piece][:].rearrange("c t (u p e) -> c t u p e", u=2, e=2),
-                in_=y_tile[piece][:].rearrange("c t (p u e) -> c t u p e", u=2, e=2),
+                out=y_words[piece][:].rearrange("c t (v p e) -> c t v p e", v=2, e=2),
+                in_=y_tile[piece][:].rearrange("c t (p v e) -> c t v p e", v=2, e=2),
             )
 
-        def turn(batch):
-            for piece in batch:
-                banks[piece] = turn_pool.tile([P, len(piece), 2, P], F32, name="turned")
+        def turn(run):
+            for piece in run:
+                if run in long_runs:
+                    banks[piece] = turn_pool.tile([P, len(piece), 2, P], F32, name="turned")
+                else:
+                    banks[piece] = acc_pool.tile([P, len(piece), 2, P], F32, name="acc")
                 words = y_words[piece][:].bitcast(F32)
                 for t in range(len(piece)):
-                    for u in range(2):
-                        nc.tensor.transpose(banks[piece][:, t, u, :], words[:, t, u * P : (u + 1) * P], ident[:])
+                    for v in range(2):
+                        nc.tensor.transpose(banks[piece][:, t, v, :], words[:, t, v * P : (v + 1) * P], ident[:])
 
-        def copy_out(batch, k):
-            piece = batch[k]
-            if k == 0:
-                tiles = sum(len(x) for x in batch)
-                y_turned[batch] = flow.tile([P, tiles * P * PACK], BF16, name="y_turned", bufs=3, align_bytes=64)
-            width = len(piece) * P * 2
-            dst = y_turned[batch][:].bitcast(F32)[:, k * width : (k + 1) * width]
+        def copy_out(piece):
+            h, i = divmod(piece[0], TILES)
+            span = span_of[h, i]
+            if i == span.start:
+                y_turned[h, span] = flow.tile([P, len(span) * P * PACK], BF16, name="y_turned", align_bytes=MX_ALIGN)
+            lo = (i - span.start) * P * 2
+            dst = y_turned[h, span][:].bitcast(F32)[:, lo : lo + len(piece) * P * 2]
             nc.scalar.copy(
-                out=dst.rearrange("p (t c u) -> p t c u", c=P, u=2), in_=banks[piece][:].rearrange("p t u c -> p t c u")
+                out=dst.rearrange("p (t c v) -> p t c v", c=P, v=2), in_=banks[piece][:].rearrange("p t v c -> p t c v")
             )
+            return [(h, span)] if i + len(piece) == span.stop else []
 
-        def quantize_y(batch):
-            h, i = divmod(batch[0][0], TILES)
-            last = batch[-1][-1] % TILES
-            cols = slice(i * P, (last + 1) * P)
+        def quantize_y(h, span):
+            cols = slice(span.start * P, span.stop * P)
             nc.vector.quantize_mx(
-                out=y_codes[h][:, cols].bitcast(FP8X4), scales=y_plane[h][:, cols], in_=y_turned[batch][:]
+                out=y_codes[h][:, cols].bitcast(FP8X4), scales=y_plane[h][:, cols], in_=y_turned[h, span][:]
             )
             dst = out_1[h].rearrange("p m t -> p (m t)")[:, cols.start * PACK : cols.stop * PACK]
             nc.sync.dma_start(out=dst.bitcast(I32), in_=y_codes[h][:, cols].bitcast(I32))
 
-        def store_scales(h, lo, hi, queues):
-            for q in range(4):
+        def store_scales(h, queues):
+            for q in range(QUADRANTS):
                 queues[q % len(queues)].dma_start(
-                    out=out_2[h, 4 * q : 4 * q + 4, lo:hi].bitcast(I32),
-                    in_=y_plane[h][32 * q : 32 * q + 4, lo:hi].bitcast(I32),
+                    out=out_2[h, 4 * q : 4 * q + 4, :].bitcast(I32),
+                    in_=y_plane[h][32 * q : 32 * q + 4, :].bitcast(I32),
                 )
 
-        full = [b for b in batches if len(b) == 2]
-        turn_step = {max(4 * n + 4, min(SLOW * n + FIRST, FAST * n + CATCH)): b for n, b in enumerate(full)}
-        for n, b in enumerate(batches[len(full) :]):
-            turn_step[UNITS - 2 + n] = b
-        assert len(turn_step) == len(batches)
+        last_long_step = long_runs[-1][-1][-1] + 1
+        turn_at = {last_long_step - RUN_SPACING * n: run for n, run in enumerate(reversed(long_runs[1:]))}
+        turn_at[FIRST_RUN_STEP] = long_runs[0]
+        for run in short_runs:
+            turn_at[run[0][-1] + 1] = run
+        round_at = {}
+        for step, run in turn_at.items():
+            for k, piece in enumerate(run):
+                round_at.setdefault(max(piece[-1] + 1, step - 2 + k), []).append((run, k))
+        copy_at, quantize_at = {}, {}
 
         for s in range(UNITS + 4):
             if s + SHR_AHEAD < UNITS:
                 scale_shift(s + SHR_AHEAD)
-            if 2 <= s <= 12 and s % 2 == 0:
-                g, part = divmod(s // 2 - 1, 2)
-                width = (HALF - LATE_VECTOR_COLS) // 2
-                interleave_w(nc.scalar.copy, g, 1, part * width, (part + 1) * width)
+            late_g, part = divmod(s - W_LATE_FROM, 3)
+            if 0 <= late_g < PASSES and part < 2:
+                interleave_w(nc.scalar.copy, late_g, 1, part * HALF // 2, (part + 1) * HALF // 2)
             if s < UNITS:
                 epilogue(s)
-            if s in (3, 7, 11) and LATE_VECTOR_COLS:
-                interleave_w(nc.vector.tensor_copy, (s - 3) // 4, 1, HALF - LATE_VECTOR_COLS, HALF)
-            if s in (5, 9, 13):
-                quantize_w((s - 5) // 4, 1)
-            if 1 <= s <= UNITS and s - 1 == piece_of[s - 1][-1]:
-                round_y(piece_of[s - 1])
-            if TILES_PER_CHUNK <= s + MM_AHEAD < UNITS:
-                for g in range(PASSES):
-                    mm_pass(s + MM_AHEAD, g)
-            for lag in (2, 1):
-                b = turn_step.get(s - lag)
-                if b is not None and lag - 1 < len(b):
-                    copy_out(b, lag - 1)
-            if s in turn_step:
-                turn(turn_step[s])
-            b = turn_step.get(s - 3)
-            if b is not None:
-                quantize_y(b)
-                if b[-1][-1] == TILES - 1:
-                    store_scales(0, 0, M, [nc.sync])
-        store_scales(1, 0, M, [nc.sync, nc.scalar])
+            if 0 <= late_g < PASSES and part == 2:
+                quantize_w(late_g, 1)
+            for run, k in round_at.get(s, []):
+                on_vector = run in short_runs or (k == 1 and s < TILES)
+                round_y(run[k], nc.vector.tensor_copy if on_vector else nc.scalar.copy)
+            for u in range(CHUNK_TILES, UNITS):
+                if s == min(u - MM_AHEAD, last_long_step):
+                    for g in range(PASSES):
+                        mm_pass(u, g)
+            for piece in copy_at.get(s, []):
+                quantize_at.setdefault(s + 2, []).extend(copy_out(piece))
+            if s in turn_at:
+                turn(turn_at[s])
+                for k, piece in enumerate(turn_at[s]):
+                    copy_at.setdefault(s + 1 + k, []).append(piece)
+            for h, span in quantize_at.get(s, []):
+                quantize_y(h, span)
+                if span.stop == TILES:
+                    store_scales(h, [nc.sync, nc.scalar] if h == HALVES - 1 else [nc.sync])

@@ -176,7 +176,7 @@ def tile_caption_projection_over_temperature_g6_kernel(
         piece_of = {u: piece for piece in pieces for u in piece}
         long_runs = [tuple(pieces[b : b + 2]) for b in range(0, len(pieces) - 3, 2)]
         short_runs = [(piece,) for piece in pieces[-3:]]
-        span_tiles = [(8, 8), (4, 4, 4, 2, 1, 1)]
+        span_tiles = [(4, 4, 4, 4), (4, 4, 4, 2, 1, 1)]
         span_of = {}
         for h in range(HALVES):
             first = 0
@@ -187,7 +187,7 @@ def tile_caption_projection_over_temperature_g6_kernel(
 
         y_tile, y_words, banks, y_turned = {}, {}, {}, {}
         y_codes = [keep.tile([P, M], U32, name="y_codes_%d" % h, align_bytes=MX_ALIGN) for h in range(HALVES)]
-        y_plane = [keep.tile([P, M], U8, name="y_plane_%d" % h, align_bytes=MX_ALIGN) for h in range(HALVES)]
+        y_plane = [keep.tile([P, CHUNK], U8, name="y_plane_%d" % h, align_bytes=MX_ALIGN) for h in range(HALVES)]
 
         def epilogue(u):
             h, i = divmod(u, TILES)
@@ -234,17 +234,17 @@ def tile_caption_projection_over_temperature_g6_kernel(
 
         def quantize_y(h, span):
             cols = slice(span.start * P, span.stop * P)
-            nc.vector.quantize_mx(
-                out=y_codes[h][:, cols].bitcast(FP8X4), scales=y_plane[h][:, cols], in_=y_turned[h, span][:]
-            )
+            n, col = divmod(cols.start, CHUNK)
+            scales = y_plane[h][4 * n :, col : col + len(span) * P]
+            nc.vector.quantize_mx(out=y_codes[h][:, cols].bitcast(FP8X4), scales=scales, in_=y_turned[h, span][:])
             dst = out_1[h].rearrange("p m t -> p (m t)")[:, cols.start * PACK : cols.stop * PACK]
             nc.sync.dma_start(out=dst.bitcast(I32), in_=y_codes[h][:, cols].bitcast(I32))
 
         def store_scales(h, queues):
             for q in range(QUADRANTS):
                 queues[q % len(queues)].dma_start(
-                    out=out_2[h, 4 * q : 4 * q + 4, :].bitcast(I32),
-                    in_=y_plane[h][32 * q : 32 * q + 4, :].bitcast(I32),
+                    out=out_2[h, 4 * q : 4 * q + 4, :].rearrange("r (n c) -> n r c", c=CHUNK).bitcast(I32),
+                    in_=y_plane[h][32 * q : 32 * q + 4 * (M // CHUNK), :].bitcast(I32),
                 )
 
         last_long_step = long_runs[-1][-1][-1] + 1

from contextlib import ExitStack

import concourse.mybir as mybir
from concourse.masks import make_identity

M, K, N = 2048, 1536, 1024
FLOPS = 2 * M * K * N

F32 = mybir.dt.float32
BF16 = mybir.dt.bfloat16
I32 = mybir.dt.int32
U32 = mybir.dt.uint32
U8 = mybir.dt.uint8
FP8X4 = mybir.dt.float8_e4m3fn_x4
ACT = mybir.ActivationFunctionType
ALU = mybir.AluOpType

P = 128
PACK = 4
QUADRANTS = 4
K_PASS = P * PACK
PASSES = K // K_PASS
HALF = 512
HALVES = N // HALF
TILES = M // P
UNITS = TILES * HALVES
CHUNK = 512
CHUNK_TILES = CHUNK // P
MX_ALIGN = 256

ACC_BANKS = 6
MM_AHEAD = 2
SHR_AHEAD = 3
SHR_BUFS = SHR_AHEAD + 2
HEAD_VECTOR_COLS = (256, 256, 320)
W_LATE_FROM = 5
FIRST_RUN_STEP = 5
RUN_SPACING = 3


def tile_caption_projection_over_temperature_g6_kernel(
    tc, x_words, x_scales, w, shift, log_tau, out_0, out_1, out_2
):
    nc = tc.nc
    with ExitStack() as ctx:
        keep = ctx.enter_context(tc.tile_pool(name="keep", bufs=1))
        flow = ctx.enter_context(tc.tile_pool(name="flow", bufs=3))
        acc_pool = ctx.enter_context(tc.psum_pool(name="acc", bufs=ACC_BANKS))
        turn_pool = ctx.enter_context(tc.psum_pool(name="turn", bufs=8 - ACC_BANKS))
        ctx.enter_context(tc.manual_schedule())

        plane_first = keep.tile([P, CHUNK], U8, align_bytes=MX_ALIGN)
        plane_rest = keep.tile([P, M - CHUNK], U8, align_bytes=MX_ALIGN)
        nc.vector.memset(plane_first[:].bitcast(I32), 0)
        nc.vector.memset(plane_rest[:].bitcast(I32), 0)

        def load_scales(plane, lo, hi):
            for q in range(QUADRANTS):
                nc.sync.dma_start(
                    out=plane[32 * q : 32 * q + 4 * PASSES, :].bitcast(I32),
                    in_=x_scales[:, 4 * q : 4 * q + 4, lo:hi].bitcast(I32),
                )

        r_rows = keep.tile([P, P], F32)
        tau_rows = keep.tile([TILES, P], BF16)
        nc.scalar.dma_start(out=tau_rows[:], in_=log_tau.rearrange("(i p) -> i p", p=P))
        shift_cols = keep.tile([P, N // P], BF16)
        nc.scalar.dma_start(out=shift_cols[:], in_=shift.rearrange("(p a) -> p a", p=P))
        ident = keep.tile([P, P], F32)
        make_identity(nc, ident[:])
        nc.scalar.activation(out=r_rows[:], in_=ident[:], func=ACT.Exp)

        w_raw, x_codes = {}, {}

        def load_w(g, h):
            raw = keep.tile([P, PACK, HALF], BF16, name="w_raw_%d_%d" % (g, h))
            rows = w[g * K_PASS : (g + 1) * K_PASS, h * HALF : (h + 1) * HALF]
            nc.sync.dma_start(out=raw[:], in_=rows.rearrange("(p t) n -> p t n", t=PACK))
            w_raw[g, h] = raw

        def load_x(c, g_lo, g_hi):
            words = keep.tile([P, g_hi - g_lo, CHUNK], U32, name="x_codes_%d_%d" % (c, g_lo), align_bytes=MX_ALIGN)
            src = x_words.rearrange("g p n t -> p g (n t)")[:, g_lo:g_hi, c * CHUNK * PACK : (c + 1) * CHUNK * PACK]
            nc.sync.dma_start(out=words[:].bitcast(I32), in_=src.bitcast(I32))
            for g in range(g_lo, g_hi):
                x_codes[c, g] = words[:, g - g_lo, :]

        load_w(0, 0)
        load_w(1, 0)
        load_x(0, 0, 1)
        load_scales(plane_first, 0, CHUNK)
        load_w(2, 0)
        load_x(0, 1, 2)
        load_x(0, 2, 3)
        load_x(1, 0, PASSES)
        load_scales(plane_rest, CHUNK, M)
        load_w(0, 1)
        load_x(2, 0, PASSES)
        load_w(1, 1)
        load_x(3, 0, PASSES)
        load_w(2, 1)

        w_grouped, w_codes, w_plane = {}, {}, {}

        def interleave_w(copy, g, h, lo, hi):
            if lo == 0:
                w_grouped[g, h] = flow.tile([P, HALF, PACK], BF16, name="w_grouped", align_bytes=MX_ALIGN)
            copy(
                out=w_grouped[g, h][:, lo:hi, :].rearrange("p (n i) t -> p n t i", i=4),
                in_=w_raw[g, h][:, :, lo:hi].rearrange("p t (n i) -> p n t i", i=4),
            )

        def quantize_w(g, h):
            codes = keep.tile([P, HALF], U32, name="w_codes_%d_%d" % (g, h), align_bytes=MX_ALIGN)
            plane = keep.tile([P, HALF], U8, name="w_plane_%d_%d" % (g, h), align_bytes=MX_ALIGN)
            nc.vector.quantize_mx(
                out=codes[:].bitcast(FP8X4), scales=plane[:], in_=w_grouped[g, h][:].rearrange("p n t -> p (n t)")
            )
            w_codes[g, h], w_plane[g, h] = codes, plane

        acc = {}

        def mm_pass(u, g):
            h, i = divmod(u, TILES)
            if g == 0:
                acc[u] = acc_pool.tile([P, HALF], F32, name="acc")
            c, col = divmod(i * P, CHUNK)
            plane, plane_col = (plane_first, col) if c == 0 else (plane_rest, i * P - CHUNK)
            nc.tensor.matmul_mx(
                out=acc[u][:],
                lhsT=x_codes[c, g][:, col : col + P].bitcast(FP8X4),
                lhsT_scale=plane[4 * g :, plane_col : plane_col + P],
                rhs=w_codes[g, h][:].bitcast(FP8X4),
                rhs_scale=w_plane[g, h][:],
                start=(g == 0),
                stop=(g == PASSES - 1),
            )

        nc.scalar.activation(out=r_rows[:TILES, :], in_=tau_rows[:], func=ACT.Exp, scale=-1.0)
        shift_words = shift_cols[:].bitcast(F32)
        shift_bank = turn_pool.tile([P, shift_words.shape[1], P], F32, name="turned")
        for a in range(shift_words.shape[1]):
            nc.tensor.transpose(shift_bank[:, a, :], shift_words[:, a : a + 1].to_broadcast([P, P]), ident[:])
        r_bank = turn_pool.tile([P, P], F32, name="turned")
        nc.tensor.transpose(r_bank[:], r_rows[:], ident[:])
        r = keep.tile([P, TILES], F32)
        shift_all = keep.tile([P, N], BF16)

        shr = {}

        def scale_shift(u):
            h, i = divmod(u, TILES)
            shr[u] = flow.tile([P, HALF], F32, name="shr", bufs=SHR_BUFS)
            src = shift_all[:, h * HALF : (h + 1) * HALF]
            if u < SHR_BUFS:
                nc.scalar.activation(out=shr[u][:], in_=src, func=ACT.Copy, scale=r[:, i : i + 1])
            else:
                nc.gpsimd.tensor_scalar(
                    out=shr[u][:], in0=src, scalar1=r[:, i : i + 1], scalar2=0.0, op0=ALU.mult, op1=ALU.add
                )

        for g in range(PASSES):
            interleave_w(nc.vector.tensor_copy, g, 0, 0, HEAD_VECTOR_COLS[g])
            interleave_w(nc.scalar.copy, g, 0, HEAD_VECTOR_COLS[g], HALF)
            if g == 1:
                nc.vector.tensor_copy(out=r[:], in_=r_bank[:, :TILES])
            quantize_w(g, 0)
            if g == 1:
                nc.scalar.copy(out=shift_all[:].bitcast(F32), in_=shift_bank[:].rearrange("p a n -> p n a"))
            for u in range(CHUNK_TILES):
                mm_pass(u, g)
        for u in range(SHR_AHEAD):
            scale_shift(u)

        pieces = [(u, u + 1) for u in range(0, UNITS - 2, 2)] + [(UNITS - 2,), (UNITS - 1,)]
        piece_of = {u: piece for piece in pieces for u in piece}
        long_runs = [tuple(pieces[b : b + 2]) for b in range(0, len(pieces) - 3, 2)]
        short_runs = [(piece,) for piece in pieces[-3:]]
        span_tiles = [(4, 4, 4, 4), (4, 4, 4, 2, 1, 1)]
        span_of = {}
        for h in range(HALVES):
            first = 0
            for count in span_tiles[h]:
                for i in range(first, first + count):
                    span_of[h, i] = range(first, first + count)
                first = first + count

        y_tile, y_words, banks, y_turned = {}, {}, {}, {}
        y_codes = [keep.tile([P, M], U32, name="y_codes_%d" % h, align_bytes=MX_ALIGN) for h in range(HALVES)]
        y_plane = [keep.tile([P, CHUNK], U8, name="y_plane_%d" % h, align_bytes=MX_ALIGN) for h in range(HALVES)]

        def epilogue(u):
            h, i = divmod(u, TILES)
            piece = piece_of[u]
            if u == piece[0]:
                y_tile[piece] = keep.tile([P, len(piece), HALF], F32, name="y_%d" % u)
            nc.vector.scalar_tensor_tensor(
                out=y_tile[piece][:, u - piece[0], :], in0=acc[u][:], scalar=r[:, i : i + 1], in1=shr[u][:],
                op0=ALU.mult, op1=ALU.add,
            )
            if u == piece[-1]:
                dst = out_0[(i + 1 - len(piece)) * P : (i + 1) * P, h * HALF : (h + 1) * HALF]
                nc.sync.dma_start(out=dst.rearrange("(t c) n -> c t n", c=P), in_=y_tile[piece][:])

        def round_y(piece, copy):
            y_words[piece] = flow.tile([P, len(piece), HALF], BF16, name="y_words", bufs=4)
            copy(
                out=y_words[piece][:].rearrange("c t (v p e) -> c t v p e", v=2, e=2),
                in_=y_tile[piece][:].rearrange("c t (p v e) -> c t v p e", v=2, e=2),
            )

        def turn(run):
            for piece in run:
                if run in long_runs:
                    banks[piece] = turn_pool.tile([P, len(piece), 2, P], F32, name="turned")
                else:
                    banks[piece] = acc_pool.tile([P, len(piece), 2, P], F32, name="acc")
                words = y_words[piece][:].bitcast(F32)
                for t in range(len(piece)):
                    for v in range(2):
                        nc.tensor.transpose(banks[piece][:, t, v, :], words[:, t, v * P : (v + 1) * P], ident[:])

        def copy_out(piece):
            h, i = divmod(piece[0], TILES)
            span = span_of[h, i]
            if i == span.start:
                y_turned[h, span] = flow.tile([P, len(span) * P * PACK], BF16, name="y_turned", align_bytes=MX_ALIGN)
            lo = (i - span.start) * P * 2
            dst = y_turned[h, span][:].bitcast(F32)[:, lo : lo + len(piece) * P * 2]
            nc.scalar.copy(
                out=dst.rearrange("p (t c v) -> p t c v", c=P, v=2), in_=banks[piece][:].rearrange("p t v c -> p t c v")
            )
            return [(h, span)] if i + len(piece) == span.stop else []

        def quantize_y(h, span):
            cols = slice(span.start * P, span.stop * P)
            n, col = divmod(cols.start, CHUNK)
            scales = y_plane[h][4 * n :, col : col + len(span) * P]
            nc.vector.quantize_mx(out=y_codes[h][:, cols].bitcast(FP8X4), scales=scales, in_=y_turned[h, span][:])
            dst = out_1[h].rearrange("p m t -> p (m t)")[:, cols.start * PACK : cols.stop * PACK]
            nc.sync.dma_start(out=dst.bitcast(I32), in_=y_codes[h][:, cols].bitcast(I32))

        def store_scales(h, queues):
            for q in range(QUADRANTS):
                queues[q % len(queues)].dma_start(
                    out=out_2[h, 4 * q : 4 * q + 4, :].rearrange("r (n c) -> n r c", c=CHUNK).bitcast(I32),
                    in_=y_plane[h][32 * q : 32 * q + 4 * (M // CHUNK), :].bitcast(I32),
                )

        last_long_step = long_runs[-1][-1][-1] + 1
        turn_at = {last_long_step - RUN_SPACING * n: run for n, run in enumerate(reversed(long_runs[1:]))}
        turn_at[FIRST_RUN_STEP] = long_runs[0]
        for run in short_runs:
            turn_at[run[0][-1] + 1] = run
        round_at = {}
        for step, run in turn_at.items():
            for k, piece in enumerate(run):
                round_at.setdefault(max(piece[-1] + 1, step - 2 + k), []).append((run, k))
        copy_at, quantize_at = {}, {}

        for s in range(UNITS + 4):
            if s + SHR_AHEAD < UNITS:
                scale_shift(s + SHR_AHEAD)
            late_g, part = divmod(s - W_LATE_FROM, 3)
            if 0 <= late_g < PASSES and part < 2:
                interleave_w(nc.scalar.copy, late_g, 1, part * HALF // 2, (part + 1) * HALF // 2)
            if s < UNITS:
                epilogue(s)
            if 0 <= late_g < PASSES and part == 2:
                quantize_w(late_g, 1)
            for run, k in round_at.get(s, []):
                on_vector = run in short_runs or (k == 1 and s < TILES)
                round_y(run[k], nc.vector.tensor_copy if on_vector else nc.scalar.copy)
            for u in range(CHUNK_TILES, UNITS):
                if s == min(u - MM_AHEAD, last_long_step):
                    for g in range(PASSES):
                        mm_pass(u, g)
            for piece in copy_at.get(s, []):
                quantize_at.setdefault(s + 2, []).extend(copy_out(piece))
            if s in turn_at:
                turn(turn_at[s])
                for k, piece in enumerate(turn_at[s]):
                    copy_at.setdefault(s + 1 + k, []).append(piece)
            for h, span in quantize_at.get(s, []):
                quantize_y(h, span)
                if span.stop == TILES:
                    store_scales(h, [nc.sync, nc.scalar] if h == HALVES - 1 else [nc.sync])
